import numpy as np
import ml_dtypes


def mxq(x, axis, fmt="e4m3"):
    dtype, down = {"e4m3": (ml_dtypes.float8_e4m3fn, 7), "e5m2": (ml_dtypes.float8_e5m2, 14)}[fmt]
    v = np.moveaxis(np.asarray(x, np.float32).astype(ml_dtypes.bfloat16).astype(np.float64), axis, -1)
    blocks = v.reshape(v.shape[:-1] + (-1, 32))
    amax = np.abs(blocks).max(-1, keepdims=True)
    byte = np.maximum(np.where(amax > 0, np.frexp(amax)[1] - 1 + 127, 0) - down, 1)
    scale = np.exp2(byte - 127.0)
    codes = (blocks / scale).astype(np.float32).astype(dtype).astype(np.float64)
    return np.moveaxis((codes * scale).reshape(v.shape), -1, axis)


WIDE = False


def mx_kscale(k):
    if not WIDE:
        return np.ones(k)
    levels = np.array([30, -30])
    if k % 512:
        return np.exp2(np.random.permutation(np.resize(levels, k // 32))).repeat(32)
    a = np.empty((k // 512, 16))
    for p in range(k // 512):
        a[p, :8] = np.random.permutation(np.resize(levels, 8))
        for g in range(8):
            far = levels[np.abs(levels - a[p, g]) >= 10]
            a[p, g + 8] = far[np.random.randint(len(far))]
    return np.exp2(a.ravel()).repeat(32)


def f64(x):
    return np.asarray(x).astype(np.float64)


def striped(idx):
    return np.tile(idx.reshape(-1, 16).T, (8, 1)).astype(np.uint16)


def unstriped(offs):
    return offs[:16].T.reshape(-1).astype(np.int64)


E2M1 = np.array([0.0, 0.5, 1.0, 1.5, 2.0, 3.0, 4.0, 6.0, -0.0, -0.5, -1.0, -1.5, -2.0, -3.0, -4.0, -6.0])


def pack_weight(w, fmt):
    k, n = w.shape
    w = f64(np.asarray(w, np.float32).astype(ml_dtypes.bfloat16)).reshape(k // 32, 32, n)
    amax = np.abs(w).max(1)
    if fmt == "e4m3":
        byte = np.frexp(amax)[1] - 1 + 127 - 7
    else:
        mant, ex = np.frexp(amax / 6.0)
        byte = np.where(mant > 0.5, ex, ex - 1) + 127
    byte = np.clip(np.where(amax > 0, byte, 1), 1, 254)
    scaled = (w * np.exp2(127.0 - byte)[:, None, :]).reshape(k, n).astype(np.float32)
    by_word = np.ascontiguousarray(scaled.reshape(k // 512, 128, 4, n).transpose(0, 1, 3, 2))
    if fmt == "e4m3":
        words = by_word.astype(ml_dtypes.float8_e4m3fn).view(np.uint8)
    else:
        c = by_word.astype(ml_dtypes.float4_e2m1fn).view(np.uint8) & 0xF
        words = (c[..., 0::2] | (c[..., 1::2] << 4)).reshape(k // 512, 128, 2 * n)
    return np.ascontiguousarray(words), np.ascontiguousarray(byte.astype(np.uint8).reshape(k // 512, 16, n))


def unpack_weight(words, scales, fmt):
    g, _, n = scales.shape
    words = np.ascontiguousarray(words).reshape(g, 128, n, -1)
    if fmt == "e4m3":
        vals = words.view(ml_dtypes.float8_e4m3fn).astype(np.float64)
    else:
        nib = np.empty((g, 128, n, 4), np.uint8)
        nib[..., 0::2] = words & 0xF
        nib[..., 1::2] = words >> 4
        vals = E2M1[nib]
    vals = vals * np.repeat(np.exp2(scales.astype(np.float64) - 127.0), 8, axis=1)[..., None]
    return vals.transpose(0, 1, 3, 2).reshape(g * 512, n)


def silu(v):
    return v / (1.0 + np.exp(-np.maximum(v, -700.0)))


def d_silu(v):
    s = 1.0 / (1.0 + np.exp(-np.maximum(v, -700.0)))
    return s * (1.0 + v * (1.0 - s))


K, T, E, C, H, N = 384, 1536, 6, 512, 512, 512


def by_expert(wq, xq):
    return np.concatenate([wq[e].T @ xq[:, e * C:(e + 1) * C] for e in range(E)], axis=1)


def setup_inputs():
    n = np.random.standard_normal
    s = mx_kscale(N)[:, None]
    u = mx_kscale(H)
    first = np.random.permutation(np.repeat(np.arange(E), T // E))
    second = (first + 1 + np.random.permutation(np.repeat(np.arange(E - 1), -(-T // (E - 1)))[:T])) % E
    while np.bincount(second, minlength=E).max() != T // E:
        load = np.bincount(second, minlength=E); hi, lo = int(load.argmax()), int(load.argmin())
        t = np.flatnonzero((second == hi) & (first != lo))[0]; second[t] = lo
    slot_token = np.empty(E * C, np.int64); pos = np.empty((2, T), np.int64); fill = np.zeros(E, np.int64)
    place = np.stack([np.random.permutation(C) for _ in range(E)])
    for r, deal in enumerate((first, second)):
        for t in np.random.permutation(T):
            e = deal[t]; j = e * C + place[e, fill[e]]; fill[e] += 1; slot_token[j] = t; pos[r, t] = j
    g = np.random.uniform(0.2, 0.8, T)
    w_slot = np.empty(E * C); w_slot[pos[0]] = g; w_slot[pos[1]] = 1.0 - g
    w2 = [pack_weight(m, "e2m1") for m in n((E, N, H)) / np.sqrt(N) / s[None] * u[None, None, :]]
    w1 = [pack_weight(m, "e2m1") for m in n((E, H, K)) / np.sqrt(H) / u[None, :, None]]
    w3 = [pack_weight(m, "e2m1") for m in n((E, H, K)) / np.sqrt(H) / u[None, :, None]]
    return {
        "dyT": (n((N, T)) * s).astype(np.float32),
        "a1": n((H, E * C)).astype(np.float32),
        "a3": n((H, E * C)).astype(np.float32),
        "w2_words": np.stack([m[0] for m in w2]),
        "w2_scales": np.stack([m[1] for m in w2]),
        "w1_words": np.stack([m[0] for m in w1]),
        "w1_scales": np.stack([m[1] for m in w1]),
        "w3_words": np.stack([m[0] for m in w3]),
        "w3_scales": np.stack([m[1] for m in w3]),
        "gate": np.tile(w_slot, (N, 1)).astype(np.float32),
        "offs": striped(slot_token),
        "pos1": striped(pos[0]),
        "pos2": striped(pos[1]),
    }


def reference(dyT, a1, a3, w2_words, w2_scales, w1_words, w1_scales, w3_words, w3_scales, gate, offs, pos1, pos2):
    idx = unstriped(offs)
    w2 = np.stack([unpack_weight(w2_words[e], w2_scales[e], "e2m1") for e in range(E)])
    w1 = np.stack([unpack_weight(w1_words[e], w1_scales[e], "e2m1") for e in range(E)])
    w3 = np.stack([unpack_weight(w3_words[e], w3_scales[e], "e2m1") for e in range(E)])
    gq = mxq(f64(gate) * f64(dyT)[:, idx], 0, "e5m2")
    dh = by_expert(w2, gq)
    da1 = dh * f64(a3) * d_silu(f64(a1))
    da3 = dh * silu(f64(a1))
    dx = by_expert(w1, mxq(da1, 0, "e5m2")) + by_expert(w3, mxq(da3, 0, "e5m2"))
    return dx[:, unstriped(pos1)] + dx[:, unstriped(pos2)]

@@ -1,0 +1,249 @@
+from contextlib import ExitStack
+
+import concourse.mybir as mybir
+
+K, T, E, C, H, N = 384, 1536, 6, 512, 512, 512
+S = E * C
+
+FLOPS = 2 * S * (N * H + 2 * H * K)
+BYTES = 4 * (N * T + 2 * H * S + S + K * T) + E * (N * H // 2 + H * K) + E * 16 * (H + 2 * K) + 2 * (S + 2 * T)
+
+F32 = mybir.dt.float32
+BF16 = mybir.dt.bfloat16
+U32 = mybir.dt.uint32
+I32 = mybir.dt.int32
+U16 = mybir.dt.uint16
+U8 = mybir.dt.uint8
+E5M2X4 = mybir.dt.float8_e5m2_x4
+E2M1X4 = mybir.dt.float4_e2m1fn_x4
+
+ADD = mybir.AluOpType.add
+SUB = mybir.AluOpType.subtract
+MULT = mybir.AluOpType.mult
+ACT = mybir.ActivationFunctionType
+
+P = 128
+W = 4
+KT = K // P
+
+
+def tile_moe_bdx_glu_silu_kernel(
+    tc, dyT, a1, a3, w2_words, w2_scales, w1_words, w1_scales, w3_words, w3_scales, gate, offs, pos1, pos2, out
+):
+    nc = tc.nc
+    with ExitStack() as ctx:
+        keep = ctx.enter_context(tc.tile_pool(name="keep", bufs=1))
+        flow = ctx.enter_context(tc.tile_pool(name="flow", bufs=2))
+        psum = ctx.enter_context(tc.psum_pool(name="psum", bufs=1))
+
+        offs_sb = keep.tile([P, S // 16], U16, name="offs_sb")
+        pos1_sb = keep.tile([P, T // 16], U16, name="pos1_sb")
+        pos2_sb = keep.tile([P, T // 16], U16, name="pos2_sb")
+        dy = []
+        for t in range(W):
+            dy_t = keep.tile([P, T], F32, name=f"dy{t}")
+            dy.append(dy_t)
+        gate_sb = keep.tile([P, S], F32, name="gate_sb")
+        dx = []
+        for kt in range(KT):
+            dx_t = keep.tile([P, S], F32, name=f"dx{kt}")
+            dx.append(dx_t)
+        w2_sb = keep.tile([P, E, 2 * H], U8, name="w2_sb", align_bytes=64)
+        w1_sb = keep.tile([P, E, 2 * K], U8, name="w1_sb", align_bytes=64)
+        w3_sb = keep.tile([P, E, 2 * K], U8, name="w3_sb", align_bytes=64)
+        w2_sc = keep.tile([P, E, H], U8, name="w2_sc", align_bytes=64)
+        w1_sc = keep.tile([P, E, K], U8, name="w1_sc", align_bytes=64)
+        w3_sc = keep.tile([P, E, K], U8, name="w3_sc", align_bytes=64)
+        w2_raw = flow.tile([P, E, 2 * H], U8, name="w2_raw", tag="dr", bufs=1, align_bytes=64)
+        w2_rawsc = flow.tile([P, E, H], U8, name="w2_rawsc", tag="da3", align_bytes=64)
+
+        warm = keep.tile([P, 1], F32, name="warm")
+        nc.vector.memset(warm[:], 0.0)
+        nc.scalar.activation(warm[:], warm[:], ACT.Silu)
+        nc.gpsimd.memset(w2_rawsc[:].rearrange("p e i -> p (e i)").bitcast(U32), 0)
+        nc.gpsimd.memset(w1_sc[:].rearrange("p e i -> p (e i)").bitcast(U32), 0)
+        nc.gpsimd.memset(w3_sc[:].rearrange("p e i -> p (e i)").bitcast(U32), 0)
+
+        dy_rows = dyT.rearrange("(p t) c -> t p c", t=W)
+        a1_rows = a1.rearrange("(p t) c -> p t c", t=W)
+        a3_rows = a3.rearrange("(p t) c -> p t c", t=W)
+
+        def load_words(dst, words, e0=0, e1=E):
+            nc.sync.dma_start(
+                out=dst[:, e0:e1].bitcast(I32), in_=words[e0:e1, 0].bitcast(I32).rearrange("e p b -> p e b")
+            )
+
+        def load_scales(dst, scales):
+            rows = scales[:, 0].bitcast(I32).rearrange("e f i -> f e i")
+            for q in range(4):
+                nc.sync.dma_start(out=dst[32 * q : 32 * q + 4].bitcast(I32), in_=rows[4 * q : 4 * q + 4])
+
+        a1_t, a3_t = {}, {}
+
+        def load_a(e):
+            cols = slice(e * C, (e + 1) * C)
+            a1_t[e] = flow.tile([P, W, C], F32, name="a1_sb", tag="a1", bufs=3)
+            nc.sync.dma_start(out=a1_t[e][:], in_=a1_rows[:, :, cols])
+            a3_t[e] = flow.tile([P, W, C], F32, name="a3_sb", tag="a3")
+            nc.sync.dma_start(out=a3_t[e][:], in_=a3_rows[:, :, cols])
+
+        def load_gate(c0, c1):
+            nc.sync.dma_start(out=gate_sb[:, c0:c1], in_=gate[:P, c0:c1])
+
+        for e in range(0, E, 2):
+            load_words(w2_raw, w2_words, e, e + 2)
+        nc.sync.dma_start(offs_sb[:], offs)
+        load_gate(0, 2 * C)
+        for t in range(W):
+            nc.sync.dma_start(out=dy[t][:], in_=dy_rows[t])
+        load_scales(w2_rawsc, w2_scales)
+        load_gate(2 * C, S)
+        load_a(0)
+        load_a(1)
+        load_words(w1_sb, w1_words)
+        load_words(w3_sb, w3_words)
+        load_scales(w1_sc, w1_scales)
+        load_scales(w3_sc, w3_scales)
+        nc.sync.dma_start(pos1_sb[:], pos1)
+        nc.sync.dma_start(pos2_sb[:], pos2)
+
+        def by_quads(tile3):
+            return tile3.rearrange("p t (c i) -> p c t i", i=4)
+
+        def into_quads(tile2):
+            return tile2.rearrange("p (c i t) -> p c t i", i=4, t=W)
+
+        g_val, g_bf = {}, {}
+
+        def gather(pair):
+            g_val[pair] = flow.tile([P, W, 2 * C], F32, name="g_val", tag="g_val", bufs=1)
+            cols = slice(pair * 2 * C, (pair + 1) * 2 * C)
+            lists = offs_sb[:, cols.start // 16 : cols.stop // 16]
+            for t in range(W):
+                nc.vector.tensor_tensor(g_val[pair][:, t, :], dy[t][:].indirect(lists), gate_sb[:, cols], MULT)
+
+        def round_g(pair):
+            g_bf[pair] = flow.tile([P, 2 * W * C], BF16, name="g_bf", tag="g_bf", bufs=1, align_bytes=64)
+            for h in range(2):
+                nc.scalar.copy(
+                    into_quads(g_bf[pair][:, h * W * C : (h + 1) * W * C]),
+                    by_quads(g_val[pair][:, :, h * C : (h + 1) * C]),
+                )
+
+        def quantize(bf, tag):
+            width = bf.shape[1] // W
+            codes = flow.tile([P, width], U32, name=tag + "_codes", tag=tag + "_codes", align_bytes=64)
+            scales = flow.tile([P, width], U8, name=tag + "_scales", tag=tag + "_scales", align_bytes=64)
+            nc.vector.quantize_mx(out=codes[:].bitcast(E5M2X4), scales=scales[:], in_=bf[:])
+            return codes, scales
+
+        th, z = {}, {}
+
+        def acts(e):
+            z[e] = flow.tile([P, W, C], F32, name="z", tag="z")
+            nc.scalar.activation(z[e][:], a1_t[e][:], ACT.Silu, scale=-1.0)
+            nc.scalar.activation(z[e][:], z[e][:], ACT.Identity, bias=1.0, scale=-1.0)
+            th[e] = flow.tile([P, W, C], F32, name="th", tag="th")
+            nc.scalar.activation(th[e][:], a1_t[e][:], ACT.Tanh, scale=0.5)
+
+        def factors(e):
+            nc.vector.tensor_tensor(z[e][:], z[e][:], a3_t[e][:], MULT)
+
+        dh, dr, da1, da3 = {}, {}, {}, {}
+
+        def first(e):
+            dh[e] = []
+            half = slice(e % 2 * C, (e % 2 + 1) * C)
+            for t in range(W):
+                dh_t = psum.tile([P, C], F32, name="dh", tag="dh", bufs=4)
+                dh[e].append(dh_t)
+                nc.tensor.matmul_mx(
+                    out=dh_t[:],
+                    lhsT=w2_sb[:, e, 2 * P * t : 2 * P * (t + 1)].bitcast(E2M1X4),
+                    lhsT_scale=w2_sc[:, e, P * t : P * (t + 1)],
+                    rhs=g_q[e // 2][0][:, half].bitcast(E5M2X4),
+                    rhs_scale=g_q[e // 2][1][:, half],
+                    start=True,
+                    stop=True,
+                )
+
+        def gated(e):
+            dr[e] = flow.tile([P, W, C], F32, name="dr", tag="dr", bufs=1, align_bytes=64)
+            for t in range(W):
+                nc.vector.scalar_tensor_tensor(dr[e][:, t, :], th[e][:, t, :], 1.0, dh[e][t][:], ADD, MULT)
+
+        def deltas(e):
+            da3[e] = flow.tile([P, W * C], BF16, name="da3", tag="da3", align_bytes=64)
+            nc.vector.tensor_tensor(into_quads(da3[e][:]), by_quads(dr[e][:]), by_quads(a1_t[e][:]), MULT)
+            da1[e] = flow.tile([P, W * C], BF16, name="da1", tag="da1", align_bytes=64)
+            nc.vector.tensor_tensor(into_quads(da1[e][:]), by_quads(dr[e][:]), by_quads(z[e][:]), MULT)
+
+        def second(e):
+            acc = []
+            for kt in range(KT):
+                acc_k = psum.tile([P, C], F32, name="acc", tag="acc", bufs=4)
+                acc.append(acc_k)
+            for i, (w, sc, q) in enumerate(((w3_sb, w3_sc, d3_q[e]), (w1_sb, w1_sc, d1_q[e]))):
+                for kt in range(KT):
+                    nc.tensor.matmul_mx(
+                        out=acc[kt][:],
+                        lhsT=w[:, e, 2 * P * kt : 2 * P * (kt + 1)].bitcast(E2M1X4),
+                        lhsT_scale=sc[:, e, P * kt : P * (kt + 1)],
+                        rhs=q[0][:].bitcast(E5M2X4),
+                        rhs_scale=q[1][:],
+                        start=i == 0,
+                        stop=i == 1,
+                    )
+            for kt in range(KT):
+                nc.scalar.activation(dx[kt][:, e * C : (e + 1) * C], acc[kt][:], ACT.Copy, scale=0.5)
+
+        g_q, d1_q, d3_q = {}, {}, {}
+
+        for e in range(0, E, 2):
+            nc.vector.tensor_copy(
+                w2_sb[:, e : e + 2].bitcast(U16).rearrange("p e (t m) -> p e t m", t=W),
+                w2_raw[:, e : e + 2].bitcast(U16).rearrange("p e (m t) -> p e t m", t=W),
+            )
+        gather(0)
+        round_g(0)
+        nc.vector.tensor_copy(
+            w2_sc[:].rearrange("p e (t m) -> p e t m", t=W),
+            w2_rawsc[:].rearrange("p e (m t) -> p e t m", t=W),
+        )
+        g_q[0] = quantize(g_bf[0], "g")
+        first(0)
+        acts(0)
+        gather(1)
+        round_g(1)
+        factors(0)
+        for e in range(E):
+            if e + 1 < E:
+                acts(e + 1)
+            if e + 2 < E:
+                load_a(e + 2)
+            if e == 2:
+                gather(2)
+                round_g(2)
+            gated(e)
+            if e + 1 < E:
+                factors(e + 1)
+            deltas(e)
+            if e % 2 == 0 and e + 2 < E:
+                g_q[e // 2 + 1] = quantize(g_bf[e // 2 + 1], "g")
+            if e + 1 < E:
+                first(e + 1)
+            d3_q[e] = quantize(da3[e], "d3")
+            d1_q[e] = quantize(da1[e], "d1")
+            second(e)
+
+        for kt in range(KT):
+            y1 = flow.tile([P, T], F32, name="y1", tag="z")
+            y2 = flow.tile([P, T], F32, name="y2", tag="th")
+            last = kt == KT - 1
+            for c0, c1 in ((0, 1024), (1024, T)) if last else ((0, T),):
+                idx = slice(c0 // 16, c1 // 16)
+                nc.vector.tensor_copy(y1[:, c0:c1], dx[kt][:].indirect(pos1_sb[:, idx]))
+                nc.vector.tensor_copy(y2[:, c0:c1], dx[kt][:].indirect(pos2_sb[:, idx]))
+                adder = nc.vector if c0 else nc.gpsimd
+                adder.tensor_tensor(y1[:, c0:c1], y1[:, c0:c1], y2[:, c0:c1], ADD)
+                nc.sync.dma_start(out=out[kt * P : (kt + 1) * P, c0:c1], in_=y1[:, c0:c1])

@@ -44,10 +44,6 @@ def tile_moe_bdx_glu_silu_kernel(
             dy_t = keep.tile([P, T], F32, name=f"dy{t}")
             dy.append(dy_t)
         gate_sb = keep.tile([P, S], F32, name="gate_sb")
-        dx = []
-        for kt in range(KT):
-            dx_t = keep.tile([P, S], F32, name=f"dx{kt}")
-            dx.append(dx_t)
         w2_sb = keep.tile([P, E, 2 * H], U8, name="w2_sb", align_bytes=64)
         w1_sb = keep.tile([P, E, 2 * K], U8, name="w1_sb", align_bytes=64)
         w3_sb = keep.tile([P, E, 2 * K], U8, name="w3_sb", align_bytes=64)
@@ -55,7 +51,7 @@ def tile_moe_bdx_glu_silu_kernel(
         w1_sc = keep.tile([P, E, K], U8, name="w1_sc", align_bytes=64)
         w3_sc = keep.tile([P, E, K], U8, name="w3_sc", align_bytes=64)
         w2_raw = flow.tile([P, E, 2 * H], U8, name="w2_raw", tag="dr", bufs=1, align_bytes=64)
-        w2_rawsc = flow.tile([P, E, H], U8, name="w2_rawsc", tag="da3", align_bytes=64)
+        w2_rawsc = flow.tile([P, E, H], U8, name="w2_rawsc", tag="da3", bufs=1, align_bytes=64)
 
         warm = keep.tile([P, 1], F32, name="warm")
         nc.vector.memset(warm[:], 0.0)
@@ -80,12 +76,13 @@ def tile_moe_bdx_glu_silu_kernel(
 
         a1_t, a3_t = {}, {}
 
-        def load_a(e):
-            cols = slice(e * C, (e + 1) * C)
+        def load_a1(e):
             a1_t[e] = flow.tile([P, W, C], F32, name="a1_sb", tag="a1", bufs=3)
-            nc.sync.dma_start(out=a1_t[e][:], in_=a1_rows[:, :, cols])
+            nc.sync.dma_start(out=a1_t[e][:], in_=a1_rows[:, :, e * C : (e + 1) * C])
+
+        def load_a3(e):
             a3_t[e] = flow.tile([P, W, C], F32, name="a3_sb", tag="a3")
-            nc.sync.dma_start(out=a3_t[e][:], in_=a3_rows[:, :, cols])
+            nc.sync.dma_start(out=a3_t[e][:], in_=a3_rows[:, :, e * C : (e + 1) * C])
 
         def load_gate(c0, c1):
             nc.sync.dma_start(out=gate_sb[:, c0:c1], in_=gate[:P, c0:c1])
@@ -96,16 +93,19 @@ def tile_moe_bdx_glu_silu_kernel(
         load_gate(0, 2 * C)
         for t in range(W):
             nc.sync.dma_start(out=dy[t][:], in_=dy_rows[t])
+        load_a1(0)
         load_scales(w2_rawsc, w2_scales)
         load_gate(2 * C, S)
-        load_a(0)
-        load_a(1)
+        load_a3(0)
+        load_a1(1)
+        load_a3(1)
         load_words(w1_sb, w1_words)
         load_words(w3_sb, w3_words)
         load_scales(w1_sc, w1_scales)
         load_scales(w3_sc, w3_scales)
         nc.sync.dma_start(pos1_sb[:], pos1)
         nc.sync.dma_start(pos2_sb[:], pos2)
+        load_a1(2)
 
         def by_quads(tile3):
             return tile3.rearrange("p t (c i) -> p c t i", i=4)
@@ -116,7 +116,7 @@ def tile_moe_bdx_glu_silu_kernel(
         g_val, g_bf = {}, {}
 
         def gather(pair):
-            g_val[pair] = flow.tile([P, W, 2 * C], F32, name="g_val", tag="g_val", bufs=1)
+            g_val[pair] = flow.tile([P, W, 2 * C], F32, name="g_val", tag="g_val" if pair else "dx0", bufs=1)
             cols = slice(pair * 2 * C, (pair + 1) * 2 * C)
             lists = offs_sb[:, cols.start // 16 : cols.stop // 16]
             for t in range(W):
@@ -130,10 +130,10 @@ def tile_moe_bdx_glu_silu_kernel(
                     by_quads(g_val[pair][:, :, h * C : (h + 1) * C]),
                 )
 
-        def quantize(bf, tag):
+        def quantize(bf, tag, bufs=1):
             width = bf.shape[1] // W
-            codes = flow.tile([P, width], U32, name=tag + "_codes", tag=tag + "_codes", align_bytes=64)
-            scales = flow.tile([P, width], U8, name=tag + "_scales", tag=tag + "_scales", align_bytes=64)
+            codes = flow.tile([P, width], U32, name=tag + "_codes", tag=tag + "_codes", bufs=bufs, align_bytes=64)
+            scales = flow.tile([P, width], U8, name=tag + "_scales", tag=tag + "_scales", bufs=bufs, align_bytes=64)
             nc.vector.quantize_mx(out=codes[:].bitcast(E5M2X4), scales=scales[:], in_=bf[:])
             return codes, scales
 
@@ -146,8 +146,15 @@ def tile_moe_bdx_glu_silu_kernel(
             th[e] = flow.tile([P, W, C], F32, name="th", tag="th")
             nc.scalar.activation(th[e][:], a1_t[e][:], ACT.Tanh, scale=0.5)
 
-        def factors(e):
-            nc.vector.tensor_tensor(z[e][:], z[e][:], a3_t[e][:], MULT)
+        x = {}
+
+        def factors_gpsimd(e):
+            x[e] = flow.tile([P, W, C], F32, name="x", tag="x", bufs=1)
+            nc.gpsimd.tensor_tensor(x[e][:, 0:1], z[e][:, 0:1], a3_t[e][:, 0:1], MULT)
+            nc.gpsimd.tensor_tensor(x[e][:, 1:2], z[e][:, 1:2], a3_t[e][:, 1:2], MULT)
+
+        def factors_vector(e):
+            nc.vector.tensor_tensor(x[e][:, 2:4], z[e][:, 2:4], a3_t[e][:, 2:4], MULT)
 
         dh, dr, da1, da3 = {}, {}, {}, {}
 
@@ -173,10 +180,10 @@ def tile_moe_bdx_glu_silu_kernel(
                 nc.vector.scalar_tensor_tensor(dr[e][:, t, :], th[e][:, t, :], 1.0, dh[e][t][:], ADD, MULT)
 
         def deltas(e):
-            da3[e] = flow.tile([P, W * C], BF16, name="da3", tag="da3", align_bytes=64)
+            da3[e] = flow.tile([P, W * C], BF16, name="da3", tag="da3", bufs=1, align_bytes=64)
             nc.vector.tensor_tensor(into_quads(da3[e][:]), by_quads(dr[e][:]), by_quads(a1_t[e][:]), MULT)
-            da1[e] = flow.tile([P, W * C], BF16, name="da1", tag="da1", align_bytes=64)
-            nc.vector.tensor_tensor(into_quads(da1[e][:]), by_quads(dr[e][:]), by_quads(z[e][:]), MULT)
+            da1[e] = flow.tile([P, W * C], BF16, name="da1", tag="da1", bufs=1, align_bytes=64)
+            nc.vector.tensor_tensor(into_quads(da1[e][:]), by_quads(dr[e][:]), by_quads(x[e][:]), MULT)
 
         def second(e):
             acc = []
@@ -204,37 +211,48 @@ def tile_moe_bdx_glu_silu_kernel(
                 w2_sb[:, e : e + 2].bitcast(U16).rearrange("p e (t m) -> p e t m", t=W),
                 w2_raw[:, e : e + 2].bitcast(U16).rearrange("p e (m t) -> p e t m", t=W),
             )
+        acts(0)
         gather(0)
         round_g(0)
         nc.vector.tensor_copy(
             w2_sc[:].rearrange("p e (t m) -> p e t m", t=W),
             w2_rawsc[:].rearrange("p e (m t) -> p e t m", t=W),
         )
-        g_q[0] = quantize(g_bf[0], "g")
-        first(0)
-        acts(0)
+        acts(1)
         gather(1)
+        g_q[0] = quantize(g_bf[0], "g", 2)
+        first(0)
         round_g(1)
-        factors(0)
+        factors_gpsimd(0)
+        factors_vector(0)
+        gated(0)
+        first(1)
+        dx = []
+        for kt in range(KT):
+            dx_t = flow.tile([P, S], F32, name=f"dx{kt}", tag=f"dx{kt}", bufs=1)
+            dx.append(dx_t)
         for e in range(E):
-            if e + 1 < E:
-                acts(e + 1)
             if e + 2 < E:
-                load_a(e + 2)
-            if e == 2:
-                gather(2)
-                round_g(2)
-            gated(e)
-            if e + 1 < E:
-                factors(e + 1)
+                load_a3(e + 2)
+                acts(e + 2)
+            if e + 3 < E:
+                load_a1(e + 3)
             deltas(e)
-            if e % 2 == 0 and e + 2 < E:
-                g_q[e // 2 + 1] = quantize(g_bf[e // 2 + 1], "g")
             if e + 1 < E:
-                first(e + 1)
+                factors_gpsimd(e + 1)
+                gated(e + 1)
+            if e == 0 or e == 2:
+                g_q[e // 2 + 1] = quantize(g_bf[e // 2 + 1], "g", 2)
+            if e + 2 < E:
+                first(e + 2)
             d3_q[e] = quantize(da3[e], "d3")
             d1_q[e] = quantize(da1[e], "d1")
             second(e)
+            if e + 1 < E:
+                factors_vector(e + 1)
+            if e == 0:
+                gather(2)
+                round_g(2)
 
         for kt in range(KT):
             y1 = flow.tile([P, T], F32, name="y1", tag="z")

@@ -123,7 +123,7 @@ def tile_moe_bdx_glu_silu_kernel(
                 nc.vector.tensor_tensor(g_val[pair][:, t, :], dy[t][:].indirect(lists), gate_sb[:, cols], MULT)
 
         def round_g(pair):
-            g_bf[pair] = flow.tile([P, 2 * W * C], BF16, name="g_bf", tag="g_bf", bufs=1, align_bytes=64)
+            g_bf[pair] = flow.tile([P, 2 * W * C], BF16, name="g_bf", tag="g_bf" if pair else "x", bufs=1, align_bytes=64)
             for h in range(2):
                 nc.scalar.copy(
                     into_quads(g_bf[pair][:, h * W * C : (h + 1) * W * C]),
@@ -148,13 +148,14 @@ def tile_moe_bdx_glu_silu_kernel(
 
         x = {}
 
+        share = 240
+
         def factors_gpsimd(e):
-            x[e] = flow.tile([P, W, C], F32, name="x", tag="x", bufs=1)
-            nc.gpsimd.tensor_tensor(x[e][:, 0:1], z[e][:, 0:1], a3_t[e][:, 0:1], MULT)
-            nc.gpsimd.tensor_tensor(x[e][:, 1:2], z[e][:, 1:2], a3_t[e][:, 1:2], MULT)
+            x[e] = flow.tile([P, W, C], F32, name="x", tag="x", bufs=1, align_bytes=64)
+            nc.gpsimd.tensor_tensor(x[e][:, :, :share], z[e][:, :, :share], a3_t[e][:, :, :share], MULT)
 
         def factors_vector(e):
-            nc.vector.tensor_tensor(x[e][:, 2:4], z[e][:, 2:4], a3_t[e][:, 2:4], MULT)
+            nc.vector.tensor_tensor(x[e][:, :, share:], z[e][:, :, share:], a3_t[e][:, :, share:], MULT)
 
         dh, dr, da1, da3 = {}, {}, {}, {}
 
@@ -180,17 +181,17 @@ def tile_moe_bdx_glu_silu_kernel(
                 nc.vector.scalar_tensor_tensor(dr[e][:, t, :], th[e][:, t, :], 1.0, dh[e][t][:], ADD, MULT)
 
         def deltas(e):
-            da3[e] = flow.tile([P, W * C], BF16, name="da3", tag="da3", bufs=1, align_bytes=64)
-            nc.vector.tensor_tensor(into_quads(da3[e][:]), by_quads(dr[e][:]), by_quads(a1_t[e][:]), MULT)
             da1[e] = flow.tile([P, W * C], BF16, name="da1", tag="da1", bufs=1, align_bytes=64)
             nc.vector.tensor_tensor(into_quads(da1[e][:]), by_quads(dr[e][:]), by_quads(x[e][:]), MULT)
+            da3[e] = flow.tile([P, W * C], BF16, name="da3", tag="da3", bufs=1, align_bytes=64)
+            nc.vector.tensor_tensor(into_quads(da3[e][:]), by_quads(dr[e][:]), by_quads(a1_t[e][:]), MULT)
 
         def second(e):
             acc = []
             for kt in range(KT):
                 acc_k = psum.tile([P, C], F32, name="acc", tag="acc", bufs=4)
                 acc.append(acc_k)
-            for i, (w, sc, q) in enumerate(((w3_sb, w3_sc, d3_q[e]), (w1_sb, w1_sc, d1_q[e]))):
+            for i, (w, sc, q) in enumerate(((w1_sb, w1_sc, d1_q[e]), (w3_sb, w3_sc, d3_q[e]))):
                 for kt in range(KT):
                     nc.tensor.matmul_mx(
                         out=acc[kt][:],
@@ -241,27 +242,33 @@ def tile_moe_bdx_glu_silu_kernel(
             if e + 1 < E:
                 factors_gpsimd(e + 1)
                 gated(e + 1)
+                factors_vector(e + 1)
             if e == 0 or e == 2:
                 g_q[e // 2 + 1] = quantize(g_bf[e // 2 + 1], "g", 2)
             if e + 2 < E:
                 first(e + 2)
-            d3_q[e] = quantize(da3[e], "d3")
             d1_q[e] = quantize(da1[e], "d1")
+            d3_q[e] = quantize(da3[e], "d3")
             second(e)
-            if e + 1 < E:
-                factors_vector(e + 1)
             if e == 0:
                 gather(2)
                 round_g(2)
 
-        for kt in range(KT):
-            y1 = flow.tile([P, T], F32, name="y1", tag="z")
-            y2 = flow.tile([P, T], F32, name="y2", tag="th")
-            last = kt == KT - 1
-            for c0, c1 in ((0, 1024), (1024, T)) if last else ((0, T),):
-                idx = slice(c0 // 16, c1 // 16)
-                nc.vector.tensor_copy(y1[:, c0:c1], dx[kt][:].indirect(pos1_sb[:, idx]))
-                nc.vector.tensor_copy(y2[:, c0:c1], dx[kt][:].indirect(pos2_sb[:, idx]))
-                adder = nc.vector if c0 else nc.gpsimd
-                adder.tensor_tensor(y1[:, c0:c1], y1[:, c0:c1], y2[:, c0:c1], ADD)
-                nc.sync.dma_start(out=out[kt * P : (kt + 1) * P, c0:c1], in_=y1[:, c0:c1])
+        pieces = [(0, 0, T), (1, 0, T), (2, 0, 1024), (2, 1024, T)]
+        y = {}
+
+        def add(kt, c0, c1):
+            y1, y2 = y[kt]
+            nc.vector.tensor_tensor(y1[:, c0:c1], y1[:, c0:c1], y2[:, c0:c1], ADD)
+            nc.sync.dma_start(out=out[kt * P : (kt + 1) * P, c0:c1], in_=y1[:, c0:c1])
+
+        for i, (kt, c0, c1) in enumerate(pieces):
+            if c0 == 0:
+                y1 = flow.tile([P, T], F32, name="y1", tag="z")
+                y2 = flow.tile([P, T], F32, name="y2", tag="th")
+                y[kt] = y1, y2
+            nc.vector.tensor_copy(y1[:, c0:c1], dx[kt][:].indirect(pos1_sb[:, c0 // 16 : c1 // 16]))
+            if i:
+                add(*pieces[i - 1])
+            nc.vector.tensor_copy(y2[:, c0:c1], dx[kt][:].indirect(pos2_sb[:, c0 // 16 : c1 // 16]))
+        add(*pieces[-1])

@@ -259,7 +259,8 @@ def tile_moe_bdx_glu_silu_kernel(
 
         def add(kt, c0, c1):
             y1, y2 = y[kt]
-            nc.vector.tensor_tensor(y1[:, c0:c1], y1[:, c0:c1], y2[:, c0:c1], ADD)
+            adder = nc.vector if (kt, c0, c1) == pieces[-1] else nc.gpsimd
+            adder.tensor_tensor(y1[:, c0:c1], y1[:, c0:c1], y2[:, c0:c1], ADD)
             nc.sync.dma_start(out=out[kt * P : (kt + 1) * P, c0:c1], in_=y1[:, c0:c1])
 
         for i, (kt, c0, c1) in enumerate(pieces):

from contextlib import ExitStack

import concourse.mybir as mybir

K, T, E, C, H, N = 384, 1536, 6, 512, 512, 512
S = E * C

FLOPS = 2 * S * (N * H + 2 * H * K)
BYTES = 4 * (N * T + 2 * H * S + S + K * T) + E * (N * H // 2 + H * K) + E * 16 * (H + 2 * K) + 2 * (S + 2 * T)

F32 = mybir.dt.float32
BF16 = mybir.dt.bfloat16
U32 = mybir.dt.uint32
I32 = mybir.dt.int32
U16 = mybir.dt.uint16
U8 = mybir.dt.uint8
E5M2X4 = mybir.dt.float8_e5m2_x4
E2M1X4 = mybir.dt.float4_e2m1fn_x4

ADD = mybir.AluOpType.add
SUB = mybir.AluOpType.subtract
MULT = mybir.AluOpType.mult
ACT = mybir.ActivationFunctionType

P = 128
W = 4
KT = K // P


def tile_moe_bdx_glu_silu_kernel(
    tc, dyT, a1, a3, w2_words, w2_scales, w1_words, w1_scales, w3_words, w3_scales, gate, offs, pos1, pos2, out
):
    nc = tc.nc
    with ExitStack() as ctx:
        keep = ctx.enter_context(tc.tile_pool(name="keep", bufs=1))
        flow = ctx.enter_context(tc.tile_pool(name="flow", bufs=2))
        psum = ctx.enter_context(tc.psum_pool(name="psum", bufs=1))

        offs_sb = keep.tile([P, S // 16], U16, name="offs_sb")
        pos1_sb = keep.tile([P, T // 16], U16, name="pos1_sb")
        pos2_sb = keep.tile([P, T // 16], U16, name="pos2_sb")
        dy = []
        for t in range(W):
            dy_t = keep.tile([P, T], F32, name=f"dy{t}")
            dy.append(dy_t)
        gate_sb = keep.tile([P, S], F32, name="gate_sb")
        w2_sb = keep.tile([P, E, 2 * H], U8, name="w2_sb", align_bytes=64)
        w1_sb = keep.tile([P, E, 2 * K], U8, name="w1_sb", align_bytes=64)
        w3_sb = keep.tile([P, E, 2 * K], U8, name="w3_sb", align_bytes=64)
        w2_sc = keep.tile([P, E, H], U8, name="w2_sc", align_bytes=64)
        w1_sc = keep.tile([P, E, K], U8, name="w1_sc", align_bytes=64)
        w3_sc = keep.tile([P, E, K], U8, name="w3_sc", align_bytes=64)
        w2_raw = flow.tile([P, E, 2 * H], U8, name="w2_raw", tag="dr", bufs=1, align_bytes=64)
        w2_rawsc = flow.tile([P, E, H], U8, name="w2_rawsc", tag="da3", bufs=1, align_bytes=64)

        warm = keep.tile([P, 1], F32, name="warm")
        nc.vector.memset(warm[:], 0.0)
        nc.scalar.activation(warm[:], warm[:], ACT.Silu)
        nc.gpsimd.memset(w2_rawsc[:].rearrange("p e i -> p (e i)").bitcast(U32), 0)
        nc.gpsimd.memset(w1_sc[:].rearrange("p e i -> p (e i)").bitcast(U32), 0)
        nc.gpsimd.memset(w3_sc[:].rearrange("p e i -> p (e i)").bitcast(U32), 0)

        dy_rows = dyT.rearrange("(p t) c -> t p c", t=W)
        a1_rows = a1.rearrange("(p t) c -> p t c", t=W)
        a3_rows = a3.rearrange("(p t) c -> p t c", t=W)

        def load_words(dst, words, e0=0, e1=E):
            nc.sync.dma_start(
                out=dst[:, e0:e1].bitcast(I32), in_=words[e0:e1, 0].bitcast(I32).rearrange("e p b -> p e b")
            )

        def load_scales(dst, scales):
            rows = scales[:, 0].bitcast(I32).rearrange("e f i -> f e i")
            for q in range(4):
                nc.sync.dma_start(out=dst[32 * q : 32 * q + 4].bitcast(I32), in_=rows[4 * q : 4 * q + 4])

        a1_t, a3_t = {}, {}

        def load_a1(e):
            a1_t[e] = flow.tile([P, W, C], F32, name="a1_sb", tag="a1", bufs=3)
            nc.sync.dma_start(out=a1_t[e][:], in_=a1_rows[:, :, e * C : (e + 1) * C])

        def load_a3(e):
            a3_t[e] = flow.tile([P, W, C], F32, name="a3_sb", tag="a3")
            nc.sync.dma_start(out=a3_t[e][:], in_=a3_rows[:, :, e * C : (e + 1) * C])

        def load_gate(c0, c1):
            nc.sync.dma_start(out=gate_sb[:, c0:c1], in_=gate[:P, c0:c1])

        for e in range(0, E, 2):
            load_words(w2_raw, w2_words, e, e + 2)
        nc.sync.dma_start(offs_sb[:], offs)
        load_gate(0, 2 * C)
        for t in range(W):
            nc.sync.dma_start(out=dy[t][:], in_=dy_rows[t])
        load_a1(0)
        load_scales(w2_rawsc, w2_scales)
        load_gate(2 * C, S)
        load_a3(0)
        load_a1(1)
        load_a3(1)
        load_words(w1_sb, w1_words)
        load_words(w3_sb, w3_words)
        load_scales(w1_sc, w1_scales)
        load_scales(w3_sc, w3_scales)
        nc.sync.dma_start(pos1_sb[:], pos1)
        nc.sync.dma_start(pos2_sb[:], pos2)
        load_a1(2)

        def by_quads(tile3):
            return tile3.rearrange("p t (c i) -> p c t i", i=4)

        def into_quads(tile2):
            return tile2.rearrange("p (c i t) -> p c t i", i=4, t=W)

        g_val, g_bf = {}, {}

        def gather(pair):
            g_val[pair] = flow.tile([P, W, 2 * C], F32, name="g_val", tag="g_val" if pair else "dx0", bufs=1)
            cols = slice(pair * 2 * C, (pair + 1) * 2 * C)
            lists = offs_sb[:, cols.start // 16 : cols.stop // 16]
            for t in range(W):
                nc.vector.tensor_tensor(g_val[pair][:, t, :], dy[t][:].indirect(lists), gate_sb[:, cols], MULT)

        def round_g(pair):
            g_bf[pair] = flow.tile([P, 2 * W * C], BF16, name="g_bf", tag="g_bf" if pair else "x", bufs=1, align_bytes=64)
            for h in range(2):
                nc.scalar.copy(
                    into_quads(g_bf[pair][:, h * W * C : (h + 1) * W * C]),
                    by_quads(g_val[pair][:, :, h * C : (h + 1) * C]),
                )

        def quantize(bf, tag, bufs=1):
            width = bf.shape[1] // W
            codes = flow.tile([P, width], U32, name=tag + "_codes", tag=tag + "_codes", bufs=bufs, align_bytes=64)
            scales = flow.tile([P, width], U8, name=tag + "_scales", tag=tag + "_scales", bufs=bufs, align_bytes=64)
            nc.vector.quantize_mx(out=codes[:].bitcast(E5M2X4), scales=scales[:], in_=bf[:])
            return codes, scales

        th, z = {}, {}

        def acts(e):
            z[e] = flow.tile([P, W, C], F32, name="z", tag="z")
            nc.scalar.activation(z[e][:], a1_t[e][:], ACT.Silu, scale=-1.0)
            nc.scalar.activation(z[e][:], z[e][:], ACT.Identity, bias=1.0, scale=-1.0)
            th[e] = flow.tile([P, W, C], F32, name="th", tag="th")
            nc.scalar.activation(th[e][:], a1_t[e][:], ACT.Tanh, scale=0.5)

        x = {}

        share = 240

        def factors_gpsimd(e):
            x[e] = flow.tile([P, W, C], F32, name="x", tag="x", bufs=1, align_bytes=64)
            nc.gpsimd.tensor_tensor(x[e][:, :, :share], z[e][:, :, :share], a3_t[e][:, :, :share], MULT)

        def factors_vector(e):
            nc.vector.tensor_tensor(x[e][:, :, share:], z[e][:, :, share:], a3_t[e][:, :, share:], MULT)

        dh, dr, da1, da3 = {}, {}, {}, {}

        def first(e):
            dh[e] = []
            half = slice(e % 2 * C, (e % 2 + 1) * C)
            for t in range(W):
                dh_t = psum.tile([P, C], F32, name="dh", tag="dh", bufs=4)
                dh[e].append(dh_t)
                nc.tensor.matmul_mx(
                    out=dh_t[:],
                    lhsT=w2_sb[:, e, 2 * P * t : 2 * P * (t + 1)].bitcast(E2M1X4),
                    lhsT_scale=w2_sc[:, e, P * t : P * (t + 1)],
                    rhs=g_q[e // 2][0][:, half].bitcast(E5M2X4),
                    rhs_scale=g_q[e // 2][1][:, half],
                    start=True,
                    stop=True,
                )

        def gated(e):
            dr[e] = flow.tile([P, W, C], F32, name="dr", tag="dr", bufs=1, align_bytes=64)
            for t in range(W):
                nc.vector.scalar_tensor_tensor(dr[e][:, t, :], th[e][:, t, :], 1.0, dh[e][t][:], ADD, MULT)

        def deltas(e):
            da1[e] = flow.tile([P, W * C], BF16, name="da1", tag="da1", bufs=1, align_bytes=64)
            nc.vector.tensor_tensor(into_quads(da1[e][:]), by_quads(dr[e][:]), by_quads(x[e][:]), MULT)
            da3[e] = flow.tile([P, W * C], BF16, name="da3", tag="da3", bufs=1, align_bytes=64)
            nc.vector.tensor_tensor(into_quads(da3[e][:]), by_quads(dr[e][:]), by_quads(a1_t[e][:]), MULT)

        def second(e):
            acc = []
            for kt in range(KT):
                acc_k = psum.tile([P, C], F32, name="acc", tag="acc", bufs=4)
                acc.append(acc_k)
            for i, (w, sc, q) in enumerate(((w1_sb, w1_sc, d1_q[e]), (w3_sb, w3_sc, d3_q[e]))):
                for kt in range(KT):
                    nc.tensor.matmul_mx(
                        out=acc[kt][:],
                        lhsT=w[:, e, 2 * P * kt : 2 * P * (kt + 1)].bitcast(E2M1X4),
                        lhsT_scale=sc[:, e, P * kt : P * (kt + 1)],
                        rhs=q[0][:].bitcast(E5M2X4),
                        rhs_scale=q[1][:],
                        start=i == 0,
                        stop=i == 1,
                    )
            for kt in range(KT):
                nc.scalar.activation(dx[kt][:, e * C : (e + 1) * C], acc[kt][:], ACT.Copy, scale=0.5)

        g_q, d1_q, d3_q = {}, {}, {}

        for e in range(0, E, 2):
            nc.vector.tensor_copy(
                w2_sb[:, e : e + 2].bitcast(U16).rearrange("p e (t m) -> p e t m", t=W),
                w2_raw[:, e : e + 2].bitcast(U16).rearrange("p e (m t) -> p e t m", t=W),
            )
        acts(0)
        gather(0)
        round_g(0)
        nc.vector.tensor_copy(
            w2_sc[:].rearrange("p e (t m) -> p e t m", t=W),
            w2_rawsc[:].rearrange("p e (m t) -> p e t m", t=W),
        )
        acts(1)
        gather(1)
        g_q[0] = quantize(g_bf[0], "g", 2)
        first(0)
        round_g(1)
        factors_gpsimd(0)
        factors_vector(0)
        gated(0)
        first(1)
        dx = []
        for kt in range(KT):
            dx_t = flow.tile([P, S], F32, name=f"dx{kt}", tag=f"dx{kt}", bufs=1)
            dx.append(dx_t)
        for e in range(E):
            if e + 2 < E:
                load_a3(e + 2)
                acts(e + 2)
            if e + 3 < E:
                load_a1(e + 3)
            deltas(e)
            if e + 1 < E:
                factors_gpsimd(e + 1)
                gated(e + 1)
                factors_vector(e + 1)
            if e == 0 or e == 2:
                g_q[e // 2 + 1] = quantize(g_bf[e // 2 + 1], "g", 2)
            if e + 2 < E:
                first(e + 2)
            d1_q[e] = quantize(da1[e], "d1")
            d3_q[e] = quantize(da3[e], "d3")
            second(e)
            if e == 0:
                gather(2)
                round_g(2)

        pieces = [(0, 0, T), (1, 0, T), (2, 0, 1024), (2, 1024, T)]
        y = {}

        def add(kt, c0, c1):
            y1, y2 = y[kt]
            adder = nc.vector if (kt, c0, c1) == pieces[-1] else nc.gpsimd
            adder.tensor_tensor(y1[:, c0:c1], y1[:, c0:c1], y2[:, c0:c1], ADD)
            nc.sync.dma_start(out=out[kt * P : (kt + 1) * P, c0:c1], in_=y1[:, c0:c1])

        for i, (kt, c0, c1) in enumerate(pieces):
            if c0 == 0:
                y1 = flow.tile([P, T], F32, name="y1", tag="z")
                y2 = flow.tile([P, T], F32, name="y2", tag="th")
                y[kt] = y1, y2
            nc.vector.tensor_copy(y1[:, c0:c1], dx[kt][:].indirect(pos1_sb[:, c0 // 16 : c1 // 16]))
            if i:
                add(*pieces[i - 1])
            nc.vector.tensor_copy(y2[:, c0:c1], dx[kt][:].indirect(pos2_sb[:, c0 // 16 : c1 // 16]))
        add(*pieces[-1])
